import numpy as np
import ml_dtypes


def mxq(x, axis, fmt="e4m3"):
    dtype, down = {"e4m3": (ml_dtypes.float8_e4m3fn, 7), "e5m2": (ml_dtypes.float8_e5m2, 14)}[fmt]
    v = np.moveaxis(np.asarray(x, np.float32).astype(ml_dtypes.bfloat16).astype(np.float64), axis, -1)
    blocks = v.reshape(v.shape[:-1] + (-1, 32))
    amax = np.abs(blocks).max(-1, keepdims=True)
    byte = np.maximum(np.where(amax > 0, np.frexp(amax)[1] - 1 + 127, 0) - down, 1)
    scale = np.exp2(byte - 127.0)
    codes = (blocks / scale).astype(np.float32).astype(dtype).astype(np.float64)
    return np.moveaxis((codes * scale).reshape(v.shape), -1, axis)


WIDE = False


def mx_kscale(k):
    if not WIDE:
        return np.ones(k)
    levels = np.array([10, -10, 5, -5, 0])
    if k % 512:
        return np.exp2(np.random.permutation(np.resize(levels, k // 32))).repeat(32)
    a = np.empty((k // 512, 16))
    for p in range(k // 512):
        a[p, :8] = np.random.permutation(np.resize(levels, 8))
        for g in range(8):
            far = levels[np.abs(levels - a[p, g]) >= 10]
            a[p, g + 8] = far[np.random.randint(len(far))]
    return np.exp2(a.ravel()).repeat(32)


def f64(x):
    return np.asarray(x).astype(np.float64)


def striped(idx):
    return np.tile(np.asarray(idx).reshape(-1, 16).T, (8, 1)).astype(np.uint16)


def unstriped(offs):
    return offs[:16].T.reshape(-1).astype(np.int64)


E2M1 = np.array([0.0, 0.5, 1.0, 1.5, 2.0, 3.0, 4.0, 6.0, -0.0, -0.5, -1.0, -1.5, -2.0, -3.0, -4.0, -6.0])


def pack_weight(w, fmt):
    k, n = w.shape
    w = f64(np.asarray(w, np.float32).astype(ml_dtypes.bfloat16)).reshape(k // 32, 32, n)
    amax = np.abs(w).max(1)
    if fmt == "e4m3":
        byte = np.frexp(amax)[1] - 1 + 127 - 7
    else:
        mant, ex = np.frexp(amax / 6.0)
        byte = np.where(mant > 0.5, ex, ex - 1) + 127
    byte = np.clip(np.where(amax > 0, byte, 1), 1, 254)
    scaled = (w * np.exp2(127.0 - byte)[:, None, :]).reshape(k, n).astype(np.float32)
    by_word = np.ascontiguousarray(scaled.reshape(k // 512, 128, 4, n).transpose(0, 1, 3, 2))
    if fmt == "e4m3":
        words = by_word.astype(ml_dtypes.float8_e4m3fn).view(np.uint8)
    else:
        c = by_word.astype(ml_dtypes.float4_e2m1fn).view(np.uint8) & 0xF
        words = (c[..., 0::2] | (c[..., 1::2] << 4)).reshape(k // 512, 128, 2 * n)
    return np.ascontiguousarray(words), np.ascontiguousarray(byte.astype(np.uint8).reshape(k // 512, 16, n))


def unpack_weight(words, scales, fmt):
    g, _, n = scales.shape
    words = np.ascontiguousarray(words).reshape(g, 128, n, -1)
    if fmt == "e4m3":
        vals = words.view(ml_dtypes.float8_e4m3fn).astype(np.float64)
    else:
        nib = np.empty((g, 128, n, 4), np.uint8)
        nib[..., 0::2] = words & 0xF
        nib[..., 1::2] = words >> 4
        vals = E2M1[nib]
    vals = vals * np.repeat(np.exp2(scales.astype(np.float64) - 127.0), 8, axis=1)[..., None]
    return vals.transpose(0, 1, 3, 2).reshape(g * 512, n)


def softplus(v):
    return np.log(1.0 + np.exp(v))


D, K, R, T, I, Q = 512, 512, 512, 2048, 512, 128


def setup_inputs():
    n = np.random.standard_normal
    idx = np.random.permutation(T)[:I]
    fd = mx_kscale(D)
    fk = mx_kscale(K)
    fi = mx_kscale(I)
    keysp = pack_weight(n((D, T)) / fd[:, None], "e4m3")
    tabp = pack_weight(n((K, T)) / fk[:, None], "e4m3")
    return {
        "query": (n((D, Q)) * 0.9 / np.sqrt(D) * fd[:, None]).astype(np.float32),
        "keys_words": keysp[0],
        "keys_scales": keysp[1],
        "th": (np.random.uniform(-0.3, 0.6, (Q, 1))).astype(np.float32),
        "reserve": (np.random.uniform(50.0, 200.0, (Q, 1))).astype(np.float32),
        "tab_words": tabp[0],
        "tab_scales": tabp[1],
        "w1": (n((K, R)) * 1 / np.sqrt(K) * fk[:, None]).astype(np.float32),
        "gain": (np.random.uniform(0.5, 2.0, (R, 1))).astype(np.float32),
        "os": (np.random.uniform(4.0, 16.0, (1, I)) * fi).astype(np.float32),
        "vs": (np.random.uniform(0.5, 2.0, (1, I)) / fi).astype(np.float32),
        "offs": striped(idx),
    }


def reference(query, keys_words, keys_scales, th, reserve, tab_words, tab_scales, w1, gain, os, vs, offs):
    idx = unstriped(offs)
    keysu = unpack_weight(keys_words, keys_scales, "e4m3")
    tabu = unpack_weight(tab_words, tab_scales, "e4m3")
    queryq = mxq(f64(query), 0, "e4m3")
    keysidxg = keysu[:, idx]
    a = queryq.T @ keysidxg
    p = softplus(a - f64(th))
    z = np.sum(p, axis=1, keepdims=True) + f64(reserve)
    w = p / z
    w1q = mxq(f64(w1), 0, "e4m3")
    tabidxg = tabu[:, idx]
    zh = w1q.T @ tabidxg
    ht = np.tanh(zh)
    hv = ht * f64(gain)
    wo1 = w * f64(os)
    wt1 = wo1.T
    hw = hv * f64(vs)
    ht1 = hw.T
    wt1q = mxq(wt1, 0, "e4m3")
    ht1q = mxq(ht1, 0, "e4m3")
    o = wt1q.T @ ht1q
    return o

@@ -1,0 +1,217 @@
+from contextlib import ExitStack
+
+import concourse.mybir as mybir
+from concourse.masks import make_identity
+
+D, K, R, T, SLOTS, Q = 512, 512, 512, 2048, 512, 128
+FLOPS = 2 * SLOTS * (D * Q + K * R + Q * R)
+
+F32 = mybir.dt.float32
+BF16 = mybir.dt.bfloat16
+I32 = mybir.dt.int32
+U32 = mybir.dt.uint32
+U16 = mybir.dt.uint16
+U8 = mybir.dt.uint8
+FP8X4 = mybir.dt.float8_e4m3fn_x4
+ACT = mybir.ActivationFunctionType
+ALU = mybir.AluOpType
+
+P = 128
+PACK = 4
+RUN = 8
+CHUNK = 128
+CHUNKS = R // CHUNK
+CAP = 24.0
+
+
+def load_dealt_rows(queue, rows, factor):
+    queue.dma_start(
+        out=rows[0:PACK, :].rearrange("t (g e) -> t g e", e=RUN),
+        in_=factor.rearrange("o (g t e) -> (o t) g e", t=PACK, e=RUN),
+    )
+
+
+def load_scale_rows(queues, plane, scales):
+    for quadrant, queue in enumerate(queues):
+        queue.dma_start(
+            out=plane[32 * quadrant : 32 * quadrant + 4, :].bitcast(I32),
+            in_=scales[0, 4 * quadrant : 4 * quadrant + 4, :].bitcast(I32),
+        )
+
+
+def tile_attend_lrgained_capped_kernel(
+    tc, query, keys_words, keys_scales, th, reserve, tab_words, tab_scales, w1, gain, slot_factor, value_scale, offs, out
+):
+    nc = tc.nc
+    with ExitStack() as ctx:
+        lists = ctx.enter_context(tc.tile_pool(name="lists", bufs=1))
+        sb = ctx.enter_context(tc.tile_pool(name="sb", bufs=1))
+        ps = ctx.enter_context(tc.psum_pool(name="ps", bufs=1))
+
+        offsets = lists.tile([P, SLOTS // 16], U16, name="offsets")
+        key_pool = sb.tile([P, T], I32, name="key_pool")
+        key_pool_scales = sb.tile([P, T], U8, name="key_pool_scales", tag="key_scales_then_words", align_bytes=64)
+        tab_pool_scales = sb.tile([P, T], U8, name="tab_pool_scales")
+        query_raw = sb.tile([P, PACK, Q], F32, name="query_raw")
+        gain_cols = sb.tile([P, PACK], F32, name="gain_cols")
+        th_col = sb.tile([P, 1], F32, name="th_col")
+        reserve_col = sb.tile([P, 1], F32, name="reserve_col")
+        vs_rows = sb.tile([P, P], F32, name="vs_rows")
+        os_rows = sb.tile([P, P], F32, name="os_rows")
+        ident = sb.tile([P, P], F32, name="ident")
+
+        nc.gpsimd.memset(key_pool_scales[:].bitcast(I32), 0)
+        nc.vector.memset(vs_rows[:], 0.0)
+        nc.vector.memset(tab_pool_scales[:].bitcast(I32), 0)
+        nc.vector.memset(os_rows[:], 0.0)
+        make_identity(nc, ident[:])
+
+        w1_raw = sb.tile([P, PACK, R], F32, name="w1_raw")
+        tab_pool = sb.tile([P, T], I32, name="tab_pool")
+        nc.sync.dma_start(offsets[:], offs)
+        nc.sync.dma_start(out=gain_cols[:], in_=gain.rearrange("(p c) o -> p (c o)", c=PACK))
+        load_dealt_rows(nc.sync, vs_rows, value_scale)
+        load_scale_rows([nc.sync] * 4, key_pool_scales, keys_scales)
+        nc.sync.dma_start(out=key_pool[:], in_=keys_words[0].rearrange("p n t -> p (n t)").bitcast(I32))
+        nc.sync.dma_start(out=query_raw[:], in_=query.rearrange("(p j) q -> p j q", j=PACK))
+        nc.sync.dma_start(out=th_col[:], in_=th)
+        load_scale_rows([nc.sync] * 4, tab_pool_scales, tab_scales)
+        nc.sync.dma_start(out=w1_raw[:], in_=w1.rearrange("(p j) r -> p j r", j=PACK))
+        nc.sync.dma_start(out=tab_pool[:], in_=tab_words[0].rearrange("p n t -> p (n t)").bitcast(I32))
+        load_dealt_rows(nc.gpsimd, os_rows, slot_factor)
+        nc.sync.dma_start(out=reserve_col[:], in_=reserve)
+
+        key_scales = sb.tile([P, SLOTS], U8, name="key_scales", align_bytes=64)
+        nc.vector.tensor_copy(key_scales[:], key_pool_scales[:].indirect(offsets[:]))
+        key_words = sb.tile([P, SLOTS], U32, name="key_words", tag="key_scales_then_words", align_bytes=64)
+        nc.vector.tensor_copy(key_words[:], key_pool[:].bitcast(U32).indirect(offsets[:]))
+
+        gain_ps = ps.tile([P, PACK, P], F32, name="gain_ps", tag="gain_out")
+        for c in range(PACK):
+            nc.tensor.transpose(gain_ps[:, c, :], gain_cols[:, c : c + 1].to_broadcast([P, P]), ident[:])
+        vs_ps = ps.tile([P, P], F32, name="vs_ps", tag="turn")
+        nc.tensor.transpose(vs_ps[:], vs_rows[:], ident[:])
+        vs_cols = sb.tile([P, PACK], F32, name="vs_cols", tag="stage", align_bytes=64)
+        nc.scalar.copy(out=vs_cols[:], in_=vs_ps[:, 0:PACK])
+        capped_th = sb.tile([P, 1], F32, name="capped_th")
+        nc.gpsimd.tensor_scalar(capped_th[:], th_col[:], CAP, 1.0, ALU.add, ALU.mult)
+
+        factors = sb.tile([P, R // PACK, PACK, PACK], F32, name="factors")
+        for t in range(PACK):
+            nc.scalar.activation(
+                out=factors[:, :, t, :], in_=gain_ps[:].rearrange("p c m -> p m c"), func=ACT.Copy,
+                scale=vs_cols[:, t : t + 1],
+            )
+
+        query_bf = sb.tile([P, Q, PACK], BF16, name="query_bf", tag="stage", align_bytes=64)
+        query_words = sb.tile([P, Q], U32, name="query_words", align_bytes=64)
+        query_scales = sb.tile([P, Q], U8, name="query_scales", align_bytes=64)
+        nc.scalar.copy(out=query_bf[:], in_=query_raw[:].rearrange("p j q -> p q j"))
+        nc.vector.quantize_mx(
+            out=query_words[:].bitcast(FP8X4), scales=query_scales[:], in_=query_bf[:].rearrange("p q j -> p (q j)")
+        )
+
+        scores = ps.tile([P, SLOTS], F32, name="scores")
+        nc.tensor.matmul_mx(
+            out=scores[:], lhsT=query_words[:].bitcast(FP8X4), lhsT_scale=query_scales[:],
+            rhs=key_words[:].bitcast(FP8X4), rhs_scale=key_scales[:], start=True, stop=True,
+        )
+        below_cap = sb.tile([P, SLOTS], F32, name="below_cap")
+        grown = sb.tile([P, SLOTS], F32, name="grown", tag="hidden0")
+        logs = sb.tile([P, SLOTS], F32, name="logs")
+        nc.scalar.activation(out=below_cap[:], in_=scores[:], func=ACT.Relu, bias=capped_th[:], scale=-1.0)
+        nc.scalar.activation(out=grown[:], in_=below_cap[:], func=ACT.Exp, bias=CAP, scale=-1.0)
+
+        nc.scalar.activation(out=logs[:], in_=grown[:], func=ACT.Ln, bias=1.0, scale=1.0)
+
+        tab_scales_listed = sb.tile([P, SLOTS], U8, name="tab_scales_listed", tag="stage", align_bytes=64)
+        tab_scales_dealt = sb.tile([P, SLOTS], U8, name="tab_scales_dealt", align_bytes=64)
+        nc.vector.tensor_copy(tab_scales_listed[:], tab_pool_scales[:].indirect(offsets[:]))
+        nc.vector.tensor_copy(
+            out=tab_scales_dealt[:].bitcast(I32).rearrange("p (t g w) -> p t g w", t=PACK, w=RUN // 4),
+            in_=tab_scales_listed[:].bitcast(I32).rearrange("p (g t w) -> p t g w", t=PACK, w=RUN // 4),
+        )
+        w1_bf = sb.tile([P, R, PACK], BF16, name="w1_bf", tag="stage", align_bytes=64)
+        w1_words = sb.tile([P, R], U32, name="w1_words", align_bytes=64)
+        w1_scales = sb.tile([P, R], U8, name="w1_scales", align_bytes=64)
+        nc.vector.tensor_copy(
+            out=w1_bf[:].rearrange("p (c i) j -> p c j i", i=4), in_=w1_raw[:].rearrange("p j (c i) -> p c j i", i=4)
+        )
+        nc.vector.quantize_mx(
+            out=w1_words[:].bitcast(FP8X4), scales=w1_scales[:], in_=w1_bf[:].rearrange("p r j -> p (r j)")
+        )
+        tab_dealt = sb.tile([P, SLOTS], U32, name="tab_dealt", align_bytes=64)
+        nc.vector.tensor_copy(
+            tab_dealt[:].rearrange("p (t g e) -> p g t e", t=PACK, e=RUN),
+            tab_pool[:].bitcast(U32).indirect(offsets[:]),
+        )
+
+        os_ps = ps.tile([P, P], F32, name="os_ps", tag="gain_out")
+        nc.tensor.transpose(os_ps[:], os_rows[:], ident[:])
+        os_cols = sb.tile([P, PACK], F32, name="os_cols")
+        nc.scalar.copy(out=os_cols[:], in_=os_ps[:, 0:PACK])
+
+        shares = sb.tile([P, SLOTS], F32, name="shares")
+        row_sum = sb.tile([P, 1], F32, name="row_sum")
+        total = sb.tile([P, 1], F32, name="total")
+        inverse = sb.tile([P, 1], F32, name="inverse")
+        nc.vector.scalar_tensor_tensor(
+            out=shares[:], in0=scores[:], scalar=th_col[:], in1=logs[:], op0=ALU.subtract, op1=ALU.max,
+            accum_out=row_sum[:],
+        )
+        nc.vector.tensor_tensor(total[:], row_sum[:], reserve_col[:], ALU.add)
+        nc.vector.reciprocal(inverse[:], total[:])
+        weights = sb.tile([P, PACK, P], F32, name="weights")
+        nc.vector.tensor_scalar(
+            weights[:].rearrange("q t (g e) -> q t g e", e=RUN),
+            shares[:].rearrange("q (g t e) -> q t g e", t=PACK, e=RUN),
+            inverse[:], None, ALU.mult,
+        )
+        weights_ps = ps.tile([P, PACK, Q], F32, name="weights_ps", tag="turn")
+        for t in range(PACK):
+            nc.tensor.transpose(weights_ps[:, t, :], weights[:, t, :], ident[:])
+        weights_bf = sb.tile([P, Q, PACK], BF16, name="weights_bf", align_bytes=64)
+        weight_words = sb.tile([P, Q], U32, name="weight_words", align_bytes=64)
+        weight_scales = sb.tile([P, Q], U8, name="weight_scales", align_bytes=64)
+        nc.vector.tensor_tensor(
+            weights_bf[:], weights_ps[:].rearrange("p t q -> p q t"),
+            os_cols[:].unsqueeze(1).to_broadcast([P, Q, PACK]), ALU.mult,
+        )
+        nc.vector.quantize_mx(
+            out=weight_words[:].bitcast(FP8X4), scales=weight_scales[:],
+            in_=weights_bf[:].rearrange("p q t -> p (q t)"),
+        )
+
+        for c in range(CHUNKS):
+            r_cols = slice(c * CHUNK, (c + 1) * CHUNK)
+            hidden_ps = ps.tile([P, PACK, CHUNK], F32, name=f"hidden_ps{c}")
+            for t in range(PACK):
+                slot_cols = slice(t * P, (t + 1) * P)
+                nc.tensor.matmul_mx(
+                    out=hidden_ps[:, t, :], lhsT=tab_dealt[:, slot_cols].bitcast(FP8X4),
+                    lhsT_scale=tab_scales_dealt[:, slot_cols], rhs=w1_words[:, r_cols].bitcast(FP8X4),
+                    rhs_scale=w1_scales[:, r_cols], start=True, stop=True,
+                )
+            hidden = sb.tile([P, CHUNK, PACK], F32, name=f"hidden{c}")
+            nc.scalar.activation(out=hidden[:], in_=hidden_ps[:].rearrange("p t r -> p r t"), func=ACT.Tanh)
+            values_bf = sb.tile([P, CHUNK, PACK], BF16, name=f"values_bf{c}", align_bytes=64)
+            groups = slice(c * CHUNK // PACK, (c + 1) * CHUNK // PACK)
+            nc.vector.tensor_tensor(
+                values_bf[:].rearrange("p (m i) t -> p m i t", i=PACK),
+                hidden[:].rearrange("p (m i) t -> p m i t", i=PACK),
+                factors[:, groups, :, :].rearrange("p m t i -> p m i t"), ALU.mult,
+            )
+            value_words = sb.tile([P, CHUNK], U32, name=f"value_words{c}", align_bytes=64)
+            value_scales = sb.tile([P, CHUNK], U8, name=f"value_scales{c}", align_bytes=64)
+            nc.vector.quantize_mx(
+                out=value_words[:].bitcast(FP8X4), scales=value_scales[:],
+                in_=values_bf[:].rearrange("p r t -> p (r t)"),
+            )
+            result_ps = ps.tile([P, CHUNK], F32, name=f"result_ps{c}", tag=("gain_out", "result")[c % 2])
+            nc.tensor.matmul_mx(
+                out=result_ps[:], lhsT=weight_words[:].bitcast(FP8X4), lhsT_scale=weight_scales[:],
+                rhs=value_words[:].bitcast(FP8X4), rhs_scale=value_scales[:], start=True, stop=True,
+            )
+            result = sb.tile([P, CHUNK], F32, name=f"result{c}")
+            nc.scalar.copy(out=result[:], in_=result_ps[:])
+            nc.sync.dma_start(out=out[:, r_cols], in_=result[:])

@@ -21,7 +21,8 @@ PACK = 4
 RUN = 8
 CHUNK = 128
 CHUNKS = R // CHUNK
-CAP = 24.0
+TAB_PLANE = 4
+FLOOR = 2.0**-60
 
 
 def load_dealt_rows(queue, rows, factor):
@@ -31,12 +32,9 @@ def load_dealt_rows(queue, rows, factor):
     )
 
 
-def load_scale_rows(queues, plane, scales):
-    for quadrant, queue in enumerate(queues):
-        queue.dma_start(
-            out=plane[32 * quadrant : 32 * quadrant + 4, :].bitcast(I32),
-            in_=scales[0, 4 * quadrant : 4 * quadrant + 4, :].bitcast(I32),
-        )
+def load_scale_rows(queues, plane, scales, first):
+    for row, queue in enumerate(queues):
+        queue.dma_start(out=plane[first + row : P : 32, :].bitcast(I32), in_=scales[0, row:16:4, :].bitcast(I32))
 
 
 def tile_attend_lrgained_capped_kernel(
@@ -51,7 +49,7 @@ def tile_attend_lrgained_capped_kernel(
         offsets = lists.tile([P, SLOTS // 16], U16, name="offsets")
         key_pool = sb.tile([P, T], I32, name="key_pool")
         key_pool_scales = sb.tile([P, T], U8, name="key_pool_scales", tag="key_scales_then_words", align_bytes=64)
-        tab_pool_scales = sb.tile([P, T], U8, name="tab_pool_scales")
+        tab_pool_scales = sb.tile([P, T], U8, name="tab_pool_scales", align_bytes=64)
         query_raw = sb.tile([P, PACK, Q], F32, name="query_raw")
         gain_cols = sb.tile([P, PACK], F32, name="gain_cols")
         th_col = sb.tile([P, 1], F32, name="th_col")
@@ -60,26 +58,30 @@ def tile_attend_lrgained_capped_kernel(
         os_rows = sb.tile([P, P], F32, name="os_rows")
         ident = sb.tile([P, P], F32, name="ident")
 
-        nc.gpsimd.memset(key_pool_scales[:].bitcast(I32), 0)
-        nc.vector.memset(vs_rows[:], 0.0)
+        nc.gpsimd.memset(vs_rows[:], 0.0)
+        nc.vector.memset(ident[:], 0.0)
+        nc.gpsimd.memset(key_pool_scales[:, T // 2 :].bitcast(I32), 0)
+        nc.vector.memset(key_pool_scales[:, : T // 2].bitcast(I32), 0)
+        make_identity(nc, ident[:], nomemset=True)
         nc.vector.memset(tab_pool_scales[:].bitcast(I32), 0)
         nc.vector.memset(os_rows[:], 0.0)
-        make_identity(nc, ident[:])
 
         w1_raw = sb.tile([P, PACK, R], F32, name="w1_raw")
-        tab_pool = sb.tile([P, T], I32, name="tab_pool")
+        tab_pool = sb.tile([P, T], I32, name="tab_pool", align_bytes=64)
         nc.sync.dma_start(offsets[:], offs)
         nc.sync.dma_start(out=gain_cols[:], in_=gain.rearrange("(p c) o -> p (c o)", c=PACK))
-        load_dealt_rows(nc.sync, vs_rows, value_scale)
-        load_scale_rows([nc.sync] * 4, key_pool_scales, keys_scales)
+        load_dealt_rows(nc.scalar, vs_rows, value_scale)
+        load_scale_rows([nc.sync, nc.sync, nc.scalar, nc.scalar], key_pool_scales, keys_scales, 0)
         nc.sync.dma_start(out=key_pool[:], in_=keys_words[0].rearrange("p n t -> p (n t)").bitcast(I32))
         nc.sync.dma_start(out=query_raw[:], in_=query.rearrange("(p j) q -> p j q", j=PACK))
         nc.sync.dma_start(out=th_col[:], in_=th)
-        load_scale_rows([nc.sync] * 4, tab_pool_scales, tab_scales)
+        load_scale_rows([nc.sync] * 4, tab_pool_scales, tab_scales, TAB_PLANE)
         nc.sync.dma_start(out=w1_raw[:], in_=w1.rearrange("(p j) r -> p j r", j=PACK))
         nc.sync.dma_start(out=tab_pool[:], in_=tab_words[0].rearrange("p n t -> p (n t)").bitcast(I32))
-        load_dealt_rows(nc.gpsimd, os_rows, slot_factor)
+        load_dealt_rows(nc.sync, os_rows, slot_factor)
         nc.sync.dma_start(out=reserve_col[:], in_=reserve)
+        warm = sb.tile([P, 1], F32, name="warm")
+        nc.scalar.activation(out=warm[:], in_=ident[:, 0:1], func=ACT.Sigmoid)
 
         key_scales = sb.tile([P, SLOTS], U8, name="key_scales", align_bytes=64)
         nc.vector.tensor_copy(key_scales[:], key_pool_scales[:].indirect(offsets[:]))
@@ -93,8 +95,6 @@ def tile_attend_lrgained_capped_kernel(
         nc.tensor.transpose(vs_ps[:], vs_rows[:], ident[:])
         vs_cols = sb.tile([P, PACK], F32, name="vs_cols", tag="stage", align_bytes=64)
         nc.scalar.copy(out=vs_cols[:], in_=vs_ps[:, 0:PACK])
-        capped_th = sb.tile([P, 1], F32, name="capped_th")
-        nc.gpsimd.tensor_scalar(capped_th[:], th_col[:], CAP, 1.0, ALU.add, ALU.mult)
 
         factors = sb.tile([P, R // PACK, PACK, PACK], F32, name="factors")
         for t in range(PACK):
@@ -106,7 +106,10 @@ def tile_attend_lrgained_capped_kernel(
         query_bf = sb.tile([P, Q, PACK], BF16, name="query_bf", tag="stage", align_bytes=64)
         query_words = sb.tile([P, Q], U32, name="query_words", align_bytes=64)
         query_scales = sb.tile([P, Q], U8, name="query_scales", align_bytes=64)
-        nc.scalar.copy(out=query_bf[:], in_=query_raw[:].rearrange("p j q -> p q j"))
+        nc.scalar.activation(
+            out=query_bf[:].rearrange("p (c i) j -> p c j i", i=4),
+            in_=query_raw[:].rearrange("p j (c i) -> p c j i", i=4), func=ACT.Copy, scale=-1.0,
+        )
         nc.vector.quantize_mx(
             out=query_words[:].bitcast(FP8X4), scales=query_scales[:], in_=query_bf[:].rearrange("p q j -> p (q j)")
         )
@@ -116,13 +119,11 @@ def tile_attend_lrgained_capped_kernel(
             out=scores[:], lhsT=query_words[:].bitcast(FP8X4), lhsT_scale=query_scales[:],
             rhs=key_words[:].bitcast(FP8X4), rhs_scale=key_scales[:], start=True, stop=True,
         )
-        below_cap = sb.tile([P, SLOTS], F32, name="below_cap")
-        grown = sb.tile([P, SLOTS], F32, name="grown", tag="hidden0")
+        grown = sb.tile([P, SLOTS], F32, name="grown", tag="hidden0", align_bytes=64)
         logs = sb.tile([P, SLOTS], F32, name="logs")
-        nc.scalar.activation(out=below_cap[:], in_=scores[:], func=ACT.Relu, bias=capped_th[:], scale=-1.0)
-        nc.scalar.activation(out=grown[:], in_=below_cap[:], func=ACT.Exp, bias=CAP, scale=-1.0)
+        nc.scalar.activation(out=grown[:], in_=scores[:], func=ACT.Sigmoid, bias=th_col[:], scale=1.0)
 
-        nc.scalar.activation(out=logs[:], in_=grown[:], func=ACT.Ln, bias=1.0, scale=1.0)
+        nc.scalar.activation(out=logs[:], in_=grown[:], func=ACT.Ln, bias=FLOOR, scale=1.0)
 
         tab_scales_listed = sb.tile([P, SLOTS], U8, name="tab_scales_listed", tag="stage", align_bytes=64)
         tab_scales_dealt = sb.tile([P, SLOTS], U8, name="tab_scales_dealt", align_bytes=64)
@@ -131,35 +132,40 @@ def tile_attend_lrgained_capped_kernel(
             out=tab_scales_dealt[:].bitcast(I32).rearrange("p (t g w) -> p t g w", t=PACK, w=RUN // 4),
             in_=tab_scales_listed[:].bitcast(I32).rearrange("p (g t w) -> p t g w", t=PACK, w=RUN // 4),
         )
-        w1_bf = sb.tile([P, R, PACK], BF16, name="w1_bf", tag="stage", align_bytes=64)
+        w1_bf = sb.tile([P, R, PACK], BF16, name="w1_bf", tag="tab_pool_scales", align_bytes=64)
         w1_words = sb.tile([P, R], U32, name="w1_words", align_bytes=64)
         w1_scales = sb.tile([P, R], U8, name="w1_scales", align_bytes=64)
-        nc.vector.tensor_copy(
-            out=w1_bf[:].rearrange("p (c i) j -> p c j i", i=4), in_=w1_raw[:].rearrange("p j (c i) -> p c j i", i=4)
-        )
-        nc.vector.quantize_mx(
-            out=w1_words[:].bitcast(FP8X4), scales=w1_scales[:], in_=w1_bf[:].rearrange("p r j -> p (r j)")
-        )
+        halves = [slice(0, R // 2), slice(R // 2, R)]
+        for half in halves:
+            nc.vector.tensor_copy(
+                out=w1_bf[:, half, :].rearrange("p (c i) j -> p c j i", i=4),
+                in_=w1_raw[:, :, half].rearrange("p j (c i) -> p c j i", i=4),
+            )
+        for half in halves:
+            nc.vector.quantize_mx(
+                out=w1_words[:, half].bitcast(FP8X4), scales=w1_scales[:, half],
+                in_=w1_bf[:, half, :].rearrange("p r j -> p (r j)"),
+            )
         tab_dealt = sb.tile([P, SLOTS], U32, name="tab_dealt", align_bytes=64)
         nc.vector.tensor_copy(
             tab_dealt[:].rearrange("p (t g e) -> p g t e", t=PACK, e=RUN),
             tab_pool[:].bitcast(U32).indirect(offsets[:]),
         )
 
-        os_ps = ps.tile([P, P], F32, name="os_ps", tag="gain_out")
-        nc.tensor.transpose(os_ps[:], os_rows[:], ident[:])
-        os_cols = sb.tile([P, PACK], F32, name="os_cols")
-        nc.scalar.copy(out=os_cols[:], in_=os_ps[:, 0:PACK])
-
-        shares = sb.tile([P, SLOTS], F32, name="shares")
-        row_sum = sb.tile([P, 1], F32, name="row_sum")
+        shares = sb.tile([P, SLOTS], F32, name="shares", tag="tab_pool", align_bytes=64)
+        row_sum = sb.tile([P, 1], F32, name="row_sum", align_bytes=64)
         total = sb.tile([P, 1], F32, name="total")
         inverse = sb.tile([P, 1], F32, name="inverse")
         nc.vector.scalar_tensor_tensor(
-            out=shares[:], in0=scores[:], scalar=th_col[:], in1=logs[:], op0=ALU.subtract, op1=ALU.max,
+            out=shares[:], in0=scores[:], scalar=th_col[:], in1=logs[:], op0=ALU.add, op1=ALU.min,
             accum_out=row_sum[:],
         )
-        nc.vector.tensor_tensor(total[:], row_sum[:], reserve_col[:], ALU.add)
+        os_ps = ps.tile([P, P], F32, name="os_ps", tag="gain_out")
+        nc.tensor.transpose(os_ps[:], os_rows[:], ident[:])
+        os_cols = sb.tile([P, PACK], F32, name="os_cols")
+        nc.vector.tensor_copy(out=os_cols[:], in_=os_ps[:, 0:PACK])
+
+        nc.vector.tensor_tensor(total[:], row_sum[:], reserve_col[:], ALU.subtract)
         nc.vector.reciprocal(inverse[:], total[:])
         weights = sb.tile([P, PACK, P], F32, name="weights")
         nc.vector.tensor_scalar(
@@ -170,43 +176,52 @@ def tile_attend_lrgained_capped_kernel(
         weights_ps = ps.tile([P, PACK, Q], F32, name="weights_ps", tag="turn")
         for t in range(PACK):
             nc.tensor.transpose(weights_ps[:, t, :], weights[:, t, :], ident[:])
-        weights_bf = sb.tile([P, Q, PACK], BF16, name="weights_bf", align_bytes=64)
         weight_words = sb.tile([P, Q], U32, name="weight_words", align_bytes=64)
         weight_scales = sb.tile([P, Q], U8, name="weight_scales", align_bytes=64)
-        nc.vector.tensor_tensor(
-            weights_bf[:], weights_ps[:].rearrange("p t q -> p q t"),
-            os_cols[:].unsqueeze(1).to_broadcast([P, Q, PACK]), ALU.mult,
-        )
-        nc.vector.quantize_mx(
-            out=weight_words[:].bitcast(FP8X4), scales=weight_scales[:],
-            in_=weights_bf[:].rearrange("p q t -> p (q t)"),
-        )
 
-        for c in range(CHUNKS):
+        def values(c):
             r_cols = slice(c * CHUNK, (c + 1) * CHUNK)
             hidden_ps = ps.tile([P, PACK, CHUNK], F32, name=f"hidden_ps{c}")
             for t in range(PACK):
                 slot_cols = slice(t * P, (t + 1) * P)
                 nc.tensor.matmul_mx(
                     out=hidden_ps[:, t, :], lhsT=tab_dealt[:, slot_cols].bitcast(FP8X4),
-                    lhsT_scale=tab_scales_dealt[:, slot_cols], rhs=w1_words[:, r_cols].bitcast(FP8X4),
+                    lhsT_scale=tab_scales_dealt[TAB_PLANE:P, slot_cols], rhs=w1_words[:, r_cols].bitcast(FP8X4),
                     rhs_scale=w1_scales[:, r_cols], start=True, stop=True,
                 )
-            hidden = sb.tile([P, CHUNK, PACK], F32, name=f"hidden{c}")
-            nc.scalar.activation(out=hidden[:], in_=hidden_ps[:].rearrange("p t r -> p r t"), func=ACT.Tanh)
-            values_bf = sb.tile([P, CHUNK, PACK], BF16, name=f"values_bf{c}", align_bytes=64)
+            hidden = sb.tile([P, CHUNK // PACK, PACK, PACK], F32, name=f"hidden{c}", align_bytes=64)
+            nc.scalar.activation(
+                out=hidden[:], in_=hidden_ps[:].rearrange("p t (m i) -> p m t i", i=PACK), func=ACT.Tanh
+            )
+            values_bf = sb.tile(
+                [P, CHUNK, PACK], BF16, name=f"values_bf{c}", tag="row_sum" if c == 0 else f"values_bf{c}",
+                align_bytes=64,
+            )
             groups = slice(c * CHUNK // PACK, (c + 1) * CHUNK // PACK)
             nc.vector.tensor_tensor(
-                values_bf[:].rearrange("p (m i) t -> p m i t", i=PACK),
-                hidden[:].rearrange("p (m i) t -> p m i t", i=PACK),
-                factors[:, groups, :, :].rearrange("p m t i -> p m i t"), ALU.mult,
+                values_bf[:].rearrange("p (m i) t -> p m t i", i=PACK), hidden[:], factors[:, groups, :, :], ALU.mult
             )
+            return values_bf
+
+        def quantised_weights():
+            weights_bf = sb.tile([P, Q, PACK], BF16, name="weights_bf", align_bytes=64)
+            nc.vector.tensor_tensor(
+                weights_bf[:], weights_ps[:].rearrange("p t q -> p q t"),
+                os_cols[:].unsqueeze(1).to_broadcast([P, Q, PACK]), ALU.mult,
+            )
+            return weights_bf
+
+        def quantise(values_bf, c):
             value_words = sb.tile([P, CHUNK], U32, name=f"value_words{c}", align_bytes=64)
             value_scales = sb.tile([P, CHUNK], U8, name=f"value_scales{c}", align_bytes=64)
             nc.vector.quantize_mx(
                 out=value_words[:].bitcast(FP8X4), scales=value_scales[:],
                 in_=values_bf[:].rearrange("p r t -> p (r t)"),
             )
+            return value_words, value_scales
+
+        def read_out(quantised, c):
+            value_words, value_scales = quantised
             result_ps = ps.tile([P, CHUNK], F32, name=f"result_ps{c}", tag=("gain_out", "result")[c % 2])
             nc.tensor.matmul_mx(
                 out=result_ps[:], lhsT=weight_words[:].bitcast(FP8X4), lhsT_scale=weight_scales[:],
@@ -214,4 +229,20 @@ def tile_attend_lrgained_capped_kernel(
             )
             result = sb.tile([P, CHUNK], F32, name=f"result{c}")
             nc.scalar.copy(out=result[:], in_=result_ps[:])
-            nc.sync.dma_start(out=out[:, r_cols], in_=result[:])
+            nc.sync.dma_start(out=out[:, c * CHUNK : (c + 1) * CHUNK], in_=result[:])
+
+        values_0 = values(0)
+        values_1 = values(1)
+        quantised_0 = quantise(values_0, 0)
+        weights_bf = quantised_weights()
+        values_2 = values(2)
+        nc.vector.quantize_mx(
+            out=weight_words[:].bitcast(FP8X4), scales=weight_scales[:],
+            in_=weights_bf[:].rearrange("p q t -> p (q t)"),
+        )
+        quantised_1 = quantise(values_1, 1)
+        values_3 = values(3)
+        read_out(quantised_0, 0)
+        read_out(quantised_1, 1)
+        read_out(quantise(values_2, 2), 2)
+        read_out(quantise(values_3, 3), 3)

from contextlib import ExitStack

import concourse.mybir as mybir
from concourse.masks import make_identity

D, K, R, T, SLOTS, Q = 512, 512, 512, 2048, 512, 128
FLOPS = 2 * SLOTS * (D * Q + K * R + Q * R)

F32 = mybir.dt.float32
BF16 = mybir.dt.bfloat16
I32 = mybir.dt.int32
U32 = mybir.dt.uint32
U16 = mybir.dt.uint16
U8 = mybir.dt.uint8
FP8X4 = mybir.dt.float8_e4m3fn_x4
ACT = mybir.ActivationFunctionType
ALU = mybir.AluOpType

P = 128
PACK = 4
RUN = 8
CHUNK = 128
CHUNKS = R // CHUNK
TAB_PLANE = 4
FLOOR = 2.0**-60


def load_dealt_rows(queue, rows, factor):
    queue.dma_start(
        out=rows[0:PACK, :].rearrange("t (g e) -> t g e", e=RUN),
        in_=factor.rearrange("o (g t e) -> (o t) g e", t=PACK, e=RUN),
    )


def load_scale_rows(queues, plane, scales, first):
    for row, queue in enumerate(queues):
        queue.dma_start(out=plane[first + row : P : 32, :].bitcast(I32), in_=scales[0, row:16:4, :].bitcast(I32))


def tile_attend_lrgained_capped_kernel(
    tc, query, keys_words, keys_scales, th, reserve, tab_words, tab_scales, w1, gain, slot_factor, value_scale, offs, out
):
    nc = tc.nc
    with ExitStack() as ctx:
        lists = ctx.enter_context(tc.tile_pool(name="lists", bufs=1))
        sb = ctx.enter_context(tc.tile_pool(name="sb", bufs=1))
        ps = ctx.enter_context(tc.psum_pool(name="ps", bufs=1))

        offsets = lists.tile([P, SLOTS // 16], U16, name="offsets")
        key_pool = sb.tile([P, T], I32, name="key_pool")
        key_pool_scales = sb.tile([P, T], U8, name="key_pool_scales", tag="key_scales_then_words", align_bytes=64)
        tab_pool_scales = sb.tile([P, T], U8, name="tab_pool_scales", align_bytes=64)
        query_raw = sb.tile([P, PACK, Q], F32, name="query_raw")
        gain_cols = sb.tile([P, PACK], F32, name="gain_cols")
        th_col = sb.tile([P, 1], F32, name="th_col")
        reserve_col = sb.tile([P, 1], F32, name="reserve_col")
        vs_rows = sb.tile([P, P], F32, name="vs_rows")
        os_rows = sb.tile([P, P], F32, name="os_rows")
        ident = sb.tile([P, P], F32, name="ident")

        nc.gpsimd.memset(vs_rows[:], 0.0)
        nc.vector.memset(ident[:], 0.0)
        nc.gpsimd.memset(key_pool_scales[:, T // 2 :].bitcast(I32), 0)
        nc.vector.memset(key_pool_scales[:, : T // 2].bitcast(I32), 0)
        make_identity(nc, ident[:], nomemset=True)
        nc.vector.memset(tab_pool_scales[:].bitcast(I32), 0)
        nc.vector.memset(os_rows[:], 0.0)

        w1_raw = sb.tile([P, PACK, R], F32, name="w1_raw")
        tab_pool = sb.tile([P, T], I32, name="tab_pool", align_bytes=64)
        nc.sync.dma_start(offsets[:], offs)
        nc.sync.dma_start(out=gain_cols[:], in_=gain.rearrange("(p c) o -> p (c o)", c=PACK))
        load_dealt_rows(nc.scalar, vs_rows, value_scale)
        load_scale_rows([nc.sync, nc.sync, nc.scalar, nc.scalar], key_pool_scales, keys_scales, 0)
        nc.sync.dma_start(out=key_pool[:], in_=keys_words[0].rearrange("p n t -> p (n t)").bitcast(I32))
        nc.sync.dma_start(out=query_raw[:], in_=query.rearrange("(p j) q -> p j q", j=PACK))
        nc.sync.dma_start(out=th_col[:], in_=th)
        load_scale_rows([nc.sync] * 4, tab_pool_scales, tab_scales, TAB_PLANE)
        nc.sync.dma_start(out=w1_raw[:], in_=w1.rearrange("(p j) r -> p j r", j=PACK))
        nc.sync.dma_start(out=tab_pool[:], in_=tab_words[0].rearrange("p n t -> p (n t)").bitcast(I32))
        load_dealt_rows(nc.sync, os_rows, slot_factor)
        nc.sync.dma_start(out=reserve_col[:], in_=reserve)
        warm = sb.tile([P, 1], F32, name="warm")
        nc.scalar.activation(out=warm[:], in_=ident[:, 0:1], func=ACT.Sigmoid)

        key_scales = sb.tile([P, SLOTS], U8, name="key_scales", align_bytes=64)
        nc.vector.tensor_copy(key_scales[:], key_pool_scales[:].indirect(offsets[:]))
        key_words = sb.tile([P, SLOTS], U32, name="key_words", tag="key_scales_then_words", align_bytes=64)
        nc.vector.tensor_copy(key_words[:], key_pool[:].bitcast(U32).indirect(offsets[:]))

        gain_ps = ps.tile([P, PACK, P], F32, name="gain_ps", tag="gain_out")
        for c in range(PACK):
            nc.tensor.transpose(gain_ps[:, c, :], gain_cols[:, c : c + 1].to_broadcast([P, P]), ident[:])
        vs_ps = ps.tile([P, P], F32, name="vs_ps", tag="turn")
        nc.tensor.transpose(vs_ps[:], vs_rows[:], ident[:])
        vs_cols = sb.tile([P, PACK], F32, name="vs_cols", tag="stage", align_bytes=64)
        nc.scalar.copy(out=vs_cols[:], in_=vs_ps[:, 0:PACK])

        factors = sb.tile([P, R // PACK, PACK, PACK], F32, name="factors")
        for t in range(PACK):
            nc.scalar.activation(
                out=factors[:, :, t, :], in_=gain_ps[:].rearrange("p c m -> p m c"), func=ACT.Copy,
                scale=vs_cols[:, t : t + 1],
            )

        query_bf = sb.tile([P, Q, PACK], BF16, name="query_bf", tag="stage", align_bytes=64)
        query_words = sb.tile([P, Q], U32, name="query_words", align_bytes=64)
        query_scales = sb.tile([P, Q], U8, name="query_scales", align_bytes=64)
        nc.scalar.activation(
            out=query_bf[:].rearrange("p (c i) j -> p c j i", i=4),
            in_=query_raw[:].rearrange("p j (c i) -> p c j i", i=4), func=ACT.Copy, scale=-1.0,
        )
        nc.vector.quantize_mx(
            out=query_words[:].bitcast(FP8X4), scales=query_scales[:], in_=query_bf[:].rearrange("p q j -> p (q j)")
        )

        scores = ps.tile([P, SLOTS], F32, name="scores")
        nc.tensor.matmul_mx(
            out=scores[:], lhsT=query_words[:].bitcast(FP8X4), lhsT_scale=query_scales[:],
            rhs=key_words[:].bitcast(FP8X4), rhs_scale=key_scales[:], start=True, stop=True,
        )
        grown = sb.tile([P, SLOTS], F32, name="grown", tag="hidden0", align_bytes=64)
        logs = sb.tile([P, SLOTS], F32, name="logs")
        nc.scalar.activation(out=grown[:], in_=scores[:], func=ACT.Sigmoid, bias=th_col[:], scale=1.0)

        nc.scalar.activation(out=logs[:], in_=grown[:], func=ACT.Ln, bias=FLOOR, scale=1.0)

        tab_scales_listed = sb.tile([P, SLOTS], U8, name="tab_scales_listed", tag="stage", align_bytes=64)
        tab_scales_dealt = sb.tile([P, SLOTS], U8, name="tab_scales_dealt", align_bytes=64)
        nc.vector.tensor_copy(tab_scales_listed[:], tab_pool_scales[:].indirect(offsets[:]))
        nc.vector.tensor_copy(
            out=tab_scales_dealt[:].bitcast(I32).rearrange("p (t g w) -> p t g w", t=PACK, w=RUN // 4),
            in_=tab_scales_listed[:].bitcast(I32).rearrange("p (g t w) -> p t g w", t=PACK, w=RUN // 4),
        )
        w1_bf = sb.tile([P, R, PACK], BF16, name="w1_bf", tag="tab_pool_scales", align_bytes=64)
        w1_words = sb.tile([P, R], U32, name="w1_words", align_bytes=64)
        w1_scales = sb.tile([P, R], U8, name="w1_scales", align_bytes=64)
        halves = [slice(0, R // 2), slice(R // 2, R)]
        for half in halves:
            nc.vector.tensor_copy(
                out=w1_bf[:, half, :].rearrange("p (c i) j -> p c j i", i=4),
                in_=w1_raw[:, :, half].rearrange("p j (c i) -> p c j i", i=4),
            )
        for half in halves:
            nc.vector.quantize_mx(
                out=w1_words[:, half].bitcast(FP8X4), scales=w1_scales[:, half],
                in_=w1_bf[:, half, :].rearrange("p r j -> p (r j)"),
            )
        tab_dealt = sb.tile([P, SLOTS], U32, name="tab_dealt", align_bytes=64)
        nc.vector.tensor_copy(
            tab_dealt[:].rearrange("p (t g e) -> p g t e", t=PACK, e=RUN),
            tab_pool[:].bitcast(U32).indirect(offsets[:]),
        )

        shares = sb.tile([P, SLOTS], F32, name="shares", tag="tab_pool", align_bytes=64)
        row_sum = sb.tile([P, 1], F32, name="row_sum", align_bytes=64)
        total = sb.tile([P, 1], F32, name="total")
        inverse = sb.tile([P, 1], F32, name="inverse")
        nc.vector.scalar_tensor_tensor(
            out=shares[:], in0=scores[:], scalar=th_col[:], in1=logs[:], op0=ALU.add, op1=ALU.min,
            accum_out=row_sum[:],
        )
        os_ps = ps.tile([P, P], F32, name="os_ps", tag="gain_out")
        nc.tensor.transpose(os_ps[:], os_rows[:], ident[:])
        os_cols = sb.tile([P, PACK], F32, name="os_cols")
        nc.vector.tensor_copy(out=os_cols[:], in_=os_ps[:, 0:PACK])

        nc.vector.tensor_tensor(total[:], row_sum[:], reserve_col[:], ALU.subtract)
        nc.vector.reciprocal(inverse[:], total[:])
        weights = sb.tile([P, PACK, P], F32, name="weights")
        nc.vector.tensor_scalar(
            weights[:].rearrange("q t (g e) -> q t g e", e=RUN),
            shares[:].rearrange("q (g t e) -> q t g e", t=PACK, e=RUN),
            inverse[:], None, ALU.mult,
        )
        weights_ps = ps.tile([P, PACK, Q], F32, name="weights_ps", tag="turn")
        for t in range(PACK):
            nc.tensor.transpose(weights_ps[:, t, :], weights[:, t, :], ident[:])
        weight_words = sb.tile([P, Q], U32, name="weight_words", align_bytes=64)
        weight_scales = sb.tile([P, Q], U8, name="weight_scales", align_bytes=64)

        def values(c):
            r_cols = slice(c * CHUNK, (c + 1) * CHUNK)
            hidden_ps = ps.tile([P, PACK, CHUNK], F32, name=f"hidden_ps{c}")
            for t in range(PACK):
                slot_cols = slice(t * P, (t + 1) * P)
                nc.tensor.matmul_mx(
                    out=hidden_ps[:, t, :], lhsT=tab_dealt[:, slot_cols].bitcast(FP8X4),
                    lhsT_scale=tab_scales_dealt[TAB_PLANE:P, slot_cols], rhs=w1_words[:, r_cols].bitcast(FP8X4),
                    rhs_scale=w1_scales[:, r_cols], start=True, stop=True,
                )
            hidden = sb.tile([P, CHUNK // PACK, PACK, PACK], F32, name=f"hidden{c}", align_bytes=64)
            nc.scalar.activation(
                out=hidden[:], in_=hidden_ps[:].rearrange("p t (m i) -> p m t i", i=PACK), func=ACT.Tanh
            )
            values_bf = sb.tile(
                [P, CHUNK, PACK], BF16, name=f"values_bf{c}", tag="row_sum" if c == 0 else f"values_bf{c}",
                align_bytes=64,
            )
            groups = slice(c * CHUNK // PACK, (c + 1) * CHUNK // PACK)
            nc.vector.tensor_tensor(
                values_bf[:].rearrange("p (m i) t -> p m t i", i=PACK), hidden[:], factors[:, groups, :, :], ALU.mult
            )
            return values_bf

        def quantised_weights():
            weights_bf = sb.tile([P, Q, PACK], BF16, name="weights_bf", align_bytes=64)
            nc.vector.tensor_tensor(
                weights_bf[:], weights_ps[:].rearrange("p t q -> p q t"),
                os_cols[:].unsqueeze(1).to_broadcast([P, Q, PACK]), ALU.mult,
            )
            return weights_bf

        def quantise(values_bf, c):
            value_words = sb.tile([P, CHUNK], U32, name=f"value_words{c}", align_bytes=64)
            value_scales = sb.tile([P, CHUNK], U8, name=f"value_scales{c}", align_bytes=64)
            nc.vector.quantize_mx(
                out=value_words[:].bitcast(FP8X4), scales=value_scales[:],
                in_=values_bf[:].rearrange("p r t -> p (r t)"),
            )
            return value_words, value_scales

        def read_out(quantised, c):
            value_words, value_scales = quantised
            result_ps = ps.tile([P, CHUNK], F32, name=f"result_ps{c}", tag=("gain_out", "result")[c % 2])
            nc.tensor.matmul_mx(
                out=result_ps[:], lhsT=weight_words[:].bitcast(FP8X4), lhsT_scale=weight_scales[:],
                rhs=value_words[:].bitcast(FP8X4), rhs_scale=value_scales[:], start=True, stop=True,
            )
            result = sb.tile([P, CHUNK], F32, name=f"result{c}")
            nc.scalar.copy(out=result[:], in_=result_ps[:])
            nc.sync.dma_start(out=out[:, c * CHUNK : (c + 1) * CHUNK], in_=result[:])

        values_0 = values(0)
        values_1 = values(1)
        quantised_0 = quantise(values_0, 0)
        weights_bf = quantised_weights()
        values_2 = values(2)
        nc.vector.quantize_mx(
            out=weight_words[:].bitcast(FP8X4), scales=weight_scales[:],
            in_=weights_bf[:].rearrange("p q t -> p (q t)"),
        )
        quantised_1 = quantise(values_1, 1)
        values_3 = values(3)
        read_out(quantised_0, 0)
        read_out(quantised_1, 1)
        read_out(quantise(values_2, 2), 2)
        read_out(quantise(values_3, 3), 3)
